import numpy as np
import ml_dtypes


def mxq(x, axis, fmt="e4m3"):
    dtype, down = {"e4m3": (ml_dtypes.float8_e4m3fn, 7), "e5m2": (ml_dtypes.float8_e5m2, 14)}[fmt]
    v = np.moveaxis(np.asarray(x, np.float32).astype(ml_dtypes.bfloat16).astype(np.float64), axis, -1)
    blocks = v.reshape(v.shape[:-1] + (-1, 32))
    amax = np.abs(blocks).max(-1, keepdims=True)
    byte = np.maximum(np.where(amax > 0, np.frexp(amax)[1] - 1 + 127, 0) - down, 1)
    scale = np.exp2(byte - 127.0)
    codes = (blocks / scale).astype(np.float32).astype(dtype).astype(np.float64)
    return np.moveaxis((codes * scale).reshape(v.shape), -1, axis)


WIDE = False


def mx_kscale(k):
    if not WIDE:
        return np.ones(k)
    levels = np.array([10, -10, 5, -5, 0])
    if k % 512:
        return np.exp2(np.random.permutation(np.resize(levels, k // 32))).repeat(32)
    a = np.empty((k // 512, 16))
    for p in range(k // 512):
        a[p, :8] = np.random.permutation(np.resize(levels, 8))
        for g in range(8):
            far = levels[np.abs(levels - a[p, g]) >= 10]
            a[p, g + 8] = far[np.random.randint(len(far))]
    return np.exp2(a.ravel()).repeat(32)


def f64(x):
    return np.asarray(x).astype(np.float64)


def striped(idx):
    return np.tile(idx.reshape(-1, 16).T, (8, 1)).astype(np.uint16)


def unstriped(offs):
    return offs[:16].T.reshape(-1).astype(np.int64)


def striped8(idx):
    return np.concatenate([x.reshape(-1, 16).T for x in idx]).astype(np.uint16)


def runs(offs, k):
    lists = np.stack([offs[16 * r : 16 * r + 16].T.reshape(-1) for r in range(8)]).astype(np.int64)
    return lists[np.arange(k) % 512 // 64]


def pack_weight(w):
    k, n = w.shape
    w = f64(np.asarray(w, np.float32).astype(ml_dtypes.bfloat16)).reshape(k // 32, 32, n)
    amax = np.abs(w).max(1)
    byte = np.clip(np.where(amax > 0, np.frexp(amax)[1] - 1 + 127 - 7, 1), 1, 254)
    scaled = (w * np.exp2(127.0 - byte)[:, None, :]).reshape(k, n).astype(np.float32)
    words = np.ascontiguousarray(scaled.reshape(k // 512, 128, 4, n).transpose(0, 1, 3, 2)).astype(ml_dtypes.float8_e4m3fn).view(np.uint8)
    return words, np.ascontiguousarray(byte.astype(np.uint8).reshape(k // 512, 16, n))


def unpack_weight(words, scales):
    g, p, n, _ = words.shape
    vals = np.ascontiguousarray(words).view(ml_dtypes.float8_e4m3fn).astype(np.float64) * np.repeat(np.exp2(scales.astype(np.float64) - 127.0), 8, axis=1)[..., None]
    return vals.transpose(0, 1, 3, 2).reshape(g * 512, n)


E2M1 = np.array([0.0, 0.5, 1.0, 1.5, 2.0, 3.0, 4.0, 6.0, -0.0, -0.5, -1.0, -1.5, -2.0, -3.0, -4.0, -6.0])


def pack_fp4(w):
    k, n = w.shape
    w = f64(np.asarray(w, np.float32).astype(ml_dtypes.bfloat16)).reshape(k // 32, 32, n)
    amax = np.abs(w).max(1)
    mant, ex = np.frexp(amax / 6.0)
    byte = np.clip(np.where(amax > 0, np.where(mant > 0.5, ex, ex - 1) + 127, 1), 1, 254)
    scaled = (w * np.exp2(127.0 - byte)[:, None, :]).reshape(k, n).astype(np.float32)
    c = np.ascontiguousarray(scaled.reshape(k // 512, 128, 4, n).transpose(0, 1, 3, 2)).astype(ml_dtypes.float4_e2m1fn).view(np.uint8) & 0xF
    words = (c[..., 0::2] | (c[..., 1::2] << 4)).reshape(k // 512, 128, 2 * n)
    return np.ascontiguousarray(words), np.ascontiguousarray(byte.astype(np.uint8).reshape(k // 512, 16, n))


def unpack_fp4(words, scales):
    g, _, n = scales.shape
    words = np.ascontiguousarray(words).reshape(g, 128, n, 2)
    nib = np.empty((g, 128, n, 4), np.uint8)
    nib[..., 0::2] = words & 0xF
    nib[..., 1::2] = words >> 4
    vals = E2M1[nib] * np.repeat(np.exp2(scales.astype(np.float64) - 127.0), 8, axis=1)[..., None]
    return vals.transpose(0, 1, 3, 2).reshape(g * 512, n)


def sigmoid(v):
    return 1.0 / (1.0 + np.exp(-np.maximum(v, -700.0)))

def planes(y):
    n, m = y.shape
    v = y.astype(np.float32).astype(ml_dtypes.bfloat16).astype(np.float64).reshape(n // 32, 32, m)
    top = np.abs(v).max(1)
    byte = np.clip(np.where(top > 0, np.frexp(top)[1] - 1 + 127 - 7, 1), 1, 254)
    codes = (v * np.exp2(127.0 - byte)[:, None, :]).reshape(n, m).astype(np.float32).astype(ml_dtypes.float8_e4m3fn).view(np.uint8)
    words = codes.reshape(n // 512, 128, 4, m).transpose(0, 1, 3, 2)
    return np.ascontiguousarray(words), np.ascontiguousarray(byte.astype(np.uint8).reshape(n // 512, 16, m))


K, T, S, N, H, U = 512, 2048, 512, 512, 512, 1024


def setup_inputs():
    n = np.random.standard_normal
    s = mx_kscale(K)[:, None]
    u = mx_kscale(H)
    packed_xT = pack_weight(n((K, T)) * s)
    packed_w1 = pack_fp4(n((K, H)) / np.sqrt(K) / s)
    packed_w2 = pack_fp4(n((K, H)) / np.sqrt(K) / s)
    packed_w3 = pack_fp4(n((H, N)) / np.sqrt(H) / u[:, None])
    return {
        "x_words": packed_xT[0],
        "x_scales": packed_xT[1],
        "w1_words": packed_w1[0],
        "w1_scales": packed_w1[1],
        "w2_words": packed_w2[0],
        "w2_scales": packed_w2[1],
        "sl": np.random.uniform(1.0, 2.0, (H, 1)).astype(np.float32),
        "th": (0.5 * n((H, 1))).astype(np.float32),
        "sl2": np.random.uniform(1.0, 2.0, (H, 1)).astype(np.float32),
        "th2": (0.5 * n((H, 1))).astype(np.float32),
        "gn": (np.random.uniform(0.5, 1.5, (H, 1)) * u[:, None]).astype(np.float32),
        "w3_words": packed_w3[0],
        "w3_scales": packed_w3[1],
        "mem": n((N, U)).astype(np.float32),
        "offs": striped(np.random.permutation(T)[:S]),
        "hz": striped8(np.random.randint(0, T, (8, S))),
        "n1": striped(np.random.permutation(S)),
        "n2": striped(np.random.permutation(S)),
        "n3": striped(np.random.permutation(U)[:S]),
    }


def reference(x_words, x_scales, w1_words, w1_scales, w2_words, w2_scales, sl, th, sl2, th2, gn, w3_words, w3_scales, mem, offs, hz, n1, n2, n3):
    old = f64(mem)[:, unstriped(n3)]
    xq = unpack_weight(x_words, x_scales)[:, unstriped(offs)]
    y = unpack_fp4(w1_words, w1_scales).T @ xq
    sg = sigmoid(f64(sl) * (y[:, unstriped(n1)] - f64(th)))
    x_hz = unpack_weight(x_words, x_scales)[np.arange(K)[:, None], runs(hz, K)]
    d = unpack_fp4(w2_words, w2_scales).T @ x_hz
    sg2 = sigmoid(f64(sl2) * (d[:, unstriped(n2)] - f64(th2)))
    z = f64(gn) * (sg * d + sg2 * y)
    h = unpack_fp4(w3_words, w3_scales).T @ mxq(z, 0, "e4m3")
    nw = old + sigmoid(h) * (h - old)
    out = f64(mem).copy()
    out[:, unstriped(n3)] = nw
    return (out,) + planes(out)

@@ -1,0 +1,295 @@
+from contextlib import ExitStack
+
+import concourse.mybir as mybir
+
+K, T, S, N, H, U = 512, 2048, 512, 512, 512, 1024
+FLOPS = 3 * 2 * 512 * 512 * 512
+
+F32 = mybir.dt.float32
+BF16 = mybir.dt.bfloat16
+I32 = mybir.dt.int32
+U32 = mybir.dt.uint32
+U16 = mybir.dt.uint16
+U8 = mybir.dt.uint8
+FP8X4 = mybir.dt.float8_e4m3fn_x4
+FP4X4 = mybir.dt.float4_e2m1fn_x4
+MULT = mybir.AluOpType.mult
+ADD = mybir.AluOpType.add
+SUB = mybir.AluOpType.subtract
+SIGMOID = mybir.ActivationFunctionType.Sigmoid
+COPY = mybir.ActivationFunctionType.Copy
+
+OPT = dict(order='w1w xw w2w w3w w1s w2s mv n1 n2 w3s n3 m0 m1 m2 m3',early=[],late=[],evacS=[0],warm=0,yhold=None,w3early=1,c='S0:a0 S1:b0 V2:a1 g00 n00 n10 g10 n01 n11 m0 m1 V3:step00 g01 n30 g11 n31 p20 p21 f2 f3',hzhold='w1_raw_s')
+P = 128
+PACK = 4
+HALF = S // 2
+QUAD = 32
+LIST_COLS = S // 16
+RUN = 4
+CHUNK = 256
+
+
+def tile_picked_twhcxbpaget_none_po_kernel(
+    tc, x_words, x_scales, w1_words, w1_scales, w2_words, w2_scales, sl, th, sl2, th2, gn,
+    w3_words, w3_scales, mem, offs, hz, n1, n2, n3, out_0, out_1, out_2,
+):
+    nc = tc.nc
+    with ExitStack() as ctx:
+        keep = ctx.enter_context(tc.tile_pool(name="keep", bufs=1))
+        psum = ctx.enter_context(tc.psum_pool(name="psum", bufs=8))
+
+        def sb(name, shape, dtype, tag=None):
+            return keep.tile(shape, dtype, name=name, tag=tag or name, align_bytes=64)
+
+        def load_list(name, src):
+            tile = sb(name, [P, LIST_COLS], U16)
+            nc.sync.dma_start(tile[:], src)
+            return tile
+
+        def half_of(lst, half):
+            return lst[:, half * (LIST_COLS // 2) : (half + 1) * (LIST_COLS // 2)]
+
+        def cols_of(half):
+            return slice(half * HALF, (half + 1) * HALF)
+
+        xs_win = sb("xs_win", [P, T], U8)
+        nc.gpsimd.memset(xs_win[:].bitcast(I32), 0)
+        hz_t = load_list("hz_t", hz)
+        offs_t = load_list("offs_t", offs)
+        xs_rows = x_scales[0].bitcast(I32)
+        xs_i32 = xs_win[:].bitcast(I32)
+        for e in range(2):
+            nc.sync.dma_start(xs_i32[e:P:16, :], xs_rows[e:16:2, :])
+        for e in range(2):
+            nc.sync.dma_start(xs_i32[2 + e : P : QUAD, :], xs_rows[2 + e : 16 : 4, :])
+
+        def load_words(name, words, queue, tag):
+            raw_w = sb(name + "_raw_w", [P, 2 * H], U8, tag)
+            queue.dma_start(raw_w[:].bitcast(I32), words[0].bitcast(I32))
+            return raw_w
+
+        def load_scales(name, scales, queue, tag):
+            raw_s = sb(name + "_raw_s", [P, H], U8, tag)
+            nc.vector.memset(raw_s[:].bitcast(I32), 0)
+            for r in range(4):
+                queue.dma_start(raw_s[:].bitcast(I32)[r:P:QUAD, :], scales[0].bitcast(I32)[r:16:4, :])
+            return raw_s
+
+        def deal_words(name, raw_w):
+            w = sb(name + "_w", [P, 2 * H], U8)
+            nc.scalar.copy(
+                w[:].bitcast(U16).rearrange("p (t m) -> p t m", t=PACK),
+                raw_w[:].bitcast(U16).rearrange("p (m t) -> p t m", t=PACK),
+            )
+            return w
+
+        def deal_scales(name, raw_s):
+            s = sb(name + "_s", [P, H], U8)
+            nc.vector.tensor_copy(
+                s[:].rearrange("p (t m) -> p t m", t=PACK),
+                raw_s[:].rearrange("p (m t) -> p t m", t=PACK),
+            )
+            return s
+
+        def load_column(name, src):
+            tile = sb(name, [P, PACK], F32)
+            nc.gpsimd.dma_start(tile[:], src.rearrange("(p t) o -> p (t o)", t=PACK))
+            return tile
+
+        sl_t = load_column("sl_t", sl)
+        th_t = load_column("th_t", th)
+        sl2_t = load_column("sl2_t", sl2)
+        th2_t = load_column("th2_t", th2)
+        gn_t = load_column("gn_t", gn)
+
+        def make_bias(name, slope, threshold):
+            prod = sb(name + "_prod", [P, PACK], F32)
+            bias = sb(name, [P, PACK], F32)
+            nc.gpsimd.tensor_tensor(prod[:], slope[:], threshold[:], MULT)
+            nc.gpsimd.tensor_scalar(bias[:], prod[:], -1.0, 0.0, MULT, ADD)
+            return bias
+
+        bias1 = make_bias("bias1", sl_t, th_t)
+        bias2 = make_bias("bias2", sl2_t, th2_t)
+        mem_rows = mem.rearrange("(p t) c -> p t c", t=PACK)
+        out_rows = out_0.rearrange("(p t) c -> p t c", t=PACK)
+        page = [sb("page%d" % t, [P, U], F32) for t in range(PACK)]
+        xw_win = sb("xw_win", [P, T], U32)
+        hz_s_raw = sb("hz_s_raw", [P, S], U8)
+        hz_s = sb("hz_s", [P, S], U8)
+        L = {}
+        if OPT.get("warm"):
+            warm = sb("warm", [P, 8], F32)
+            nc.vector.memset(warm[:, 0:1], 0.0)
+            nc.scalar.activation(warm[:, 1:2], warm[:, 0:1], SIGMOID)
+        for item in OPT["order"].split():
+            if item == "xw":
+                nc.sync.dma_start(xw_win[:].bitcast(I32), x_words[0].rearrange("p c r -> p (c r)").bitcast(I32))
+            elif item[0] == "m" and item != "mv":
+                nc.sync.dma_start(page[int(item[1])][:], mem_rows[:, int(item[1]), :])
+            elif item[0] == "n":
+                L[item] = load_list(item + "_t", {"n1": n1, "n2": n2, "n3": n3}[item])
+            elif item == "mv":
+                nc.vector.tensor_copy(hz_s_raw[:], xs_win[:].indirect(hz_t[:]))
+                nc.vector.tensor_copy(hz_s[:].bitcast(I32), hz_s_raw[:].bitcast(I32))
+                for e in range(2):
+                    nc.sync.dma_start(hz_s[:].bitcast(I32)[2 + e : P : QUAD, :], hz_s_raw[:].bitcast(I32)[16 + e : P : QUAD, :])
+            elif item[2] == "w":
+                L[item] = load_words(item[:2], {"w1": w1_words, "w2": w2_words, "w3": w3_words}[item[:2]], nc.sync, None)
+            else:
+                L[item] = load_scales(item[:2], {"w1": w1_scales, "w2": w2_scales, "w3": w3_scales}[item[:2]], nc.sync, None)
+        n1_t, n2_t, n3_t = L["n1"], L["n2"], L["n3"]
+        raw1_w, raw2_w, raw3_w, raw1_s, raw2_s, raw3_s = L["w1w"], L["w2w"], L["w3w"], L["w1s"], L["w2s"], L["w3s"]
+
+        tok_s = sb("tok_s", [P, S], U8)
+        nc.vector.tensor_copy(tok_s[:], xs_win[:].indirect(offs_t[:]))
+        tok_w = sb("tok_w", [P, S], U32)
+        nc.vector.tensor_copy(tok_w[:], xw_win[:].indirect(offs_t[:]))
+        old = {}
+        w1 = (deal_words("w1", raw1_w), deal_scales("w1", raw1_s))
+        w2 = (deal_words("w2", raw2_w), deal_scales("w2", raw2_s))
+        hz_w = sb("hz_w", [P, S], U32, OPT.get("hzhold", "w2_raw_s"))
+        nc.vector.tensor_copy(hz_w[:], xw_win[:].indirect(hz_t[:]))
+        if OPT.get("w3early"):
+            w3_w = deal_words("w3", raw3_w)
+        olds = {}
+
+        def fetch(t, eng, tag=None):
+            old[t] = sb("old%d" % t, [P, S], F32, tag)
+            if eng == "S":
+                nc.scalar.activation(old[t][:], page[t][:].indirect(n3_t[:]), COPY)
+            else:
+                nc.vector.tensor_copy(old[t][:], page[t][:].indirect(n3_t[:]))
+
+        for t in OPT["early"]:
+            fetch(t, "S")
+
+        def product(out, weight, t, codes, scales):
+            w, s = weight
+            nc.tensor.matmul_mx(
+                out=out,
+                lhsT=w[:, 2 * P * t : 2 * P * (t + 1)].bitcast(FP4X4),
+                lhsT_scale=s[:, P * t : P * (t + 1)],
+                rhs=codes.bitcast(FP8X4),
+                rhs_scale=scales,
+                start=True,
+                stop=True,
+            )
+
+        y = [sb("y%d" % t, [P, S], F32, "w2_raw_s" if t == OPT.get("yhold") else None) for t in range(PACK)]
+        d = [sb("d%d" % t, [P, S], F32) for t in range(PACK)]
+        for t in range(PACK):
+            bank = psum.tile([P, S], F32, tag="bank", name="y_bank")
+            product(bank[:], w1, t, tok_w[:], tok_s[:])
+            if t in OPT["evacS"]:
+                nc.scalar.copy(y[t][:], bank[:])
+            else:
+                nc.vector.tensor_copy(y[t][:], bank[:])
+        for t in range(PACK):
+            bank = psum.tile([P, S], F32, tag="bank", name="d_bank")
+            product(bank[:], w2, t, hz_w[:], hz_s[:])
+            nc.vector.tensor_copy(d[t][:], bank[:])
+        if not OPT.get("w3early"):
+            w3_w = deal_words("w3", raw3_w)
+        w3 = (w3_w, deal_scales("w3", raw3_s))
+        sg = sb("sg", [P, PACK, HALF], F32)
+        sg2 = sb("sg2", [P, PACK, HALF], F32)
+
+        h_banks = {}
+
+        def hidden(half):
+            cols = cols_of(half)
+            a = sb("a%d" % half, [P, PACK, HALF], F32)
+            b = sb("b%d" % half, [P, PACK, HALF], F32)
+            for t in range(PACK):
+                nc.scalar.activation(sg[:, t, :], y[t][:].indirect(half_of(n1_t, half)), SIGMOID,
+                                     bias=bias1[:, t : t + 1], scale=sl_t[:, t : t + 1])
+            for t in range(PACK):
+                nc.scalar.activation(sg2[:, t, :], d[t][:].indirect(half_of(n2_t, half)), SIGMOID,
+                                     bias=bias2[:, t : t + 1], scale=sl2_t[:, t : t + 1])
+            for t in range(PACK):
+                nc.vector.scalar_tensor_tensor(a[:, t, :], sg[:, t, :], gn_t[:, t : t + 1], d[t][:, cols], MULT, MULT)
+            for t in range(PACK):
+                nc.vector.scalar_tensor_tensor(b[:, t, :], sg2[:, t, :], gn_t[:, t : t + 1], y[t][:, cols], MULT, MULT)
+            z = sb("z%d" % half, [P, HALF, PACK], BF16)
+            nc.vector.tensor_tensor(
+                z[:].rearrange("p (c i) t -> p c t i", i=RUN),
+                a[:].rearrange("p t (c i) -> p c t i", i=RUN),
+                b[:].rearrange("p t (c i) -> p c t i", i=RUN),
+                ADD,
+            )
+            z_w = sb("z_w%d" % half, [P, HALF], U32)
+            z_s = sb("z_s%d" % half, [P, HALF], U8)
+            nc.vector.quantize_mx(out=z_w[:].bitcast(FP8X4), scales=z_s[:], in_=z[:].rearrange("p c t -> p (c t)"))
+            for pair in range(2):
+                bank = psum.tile([P, 2, HALF], F32, tag="bank", name="h_bank")
+                for u in range(2):
+                    product(bank[:, u, :], w3, 2 * pair + u, z_w[:], z_s[:])
+                h_banks[half, pair] = bank
+
+        planes = sb("planes", [P, PACK, U], F32)
+        steps = {}
+
+        def gate_step(half, pair):
+            cols = cols_of(half)
+            bank = h_banks[half, pair]
+            gate = sb("gate%d%d" % (half, pair), [P, 2, HALF], F32)
+            diff = sb("diff%d%d" % (half, pair), [P, 2, HALF], F32, "b1" if (half, pair) == (0, 0) else None)
+            step = sb("step%d%d" % (half, pair), [P, 2, HALF], F32)
+            nc.scalar.activation(gate[:], bank[:], SIGMOID)
+            for u in range(2):
+                nc.vector.tensor_tensor(diff[:, u, :], bank[:, u, :], old[2 * pair + u][:, cols], SUB)
+            nc.vector.tensor_tensor(step[:], gate[:], diff[:], MULT)
+            steps[half, pair] = step
+
+        def new_values(t, half):
+            new = sb("new%d%d" % (half, t), [P, HALF], F32)
+            nc.vector.tensor_tensor(new[:], old[t][:, cols_of(half)], steps[half, t // 2][:, t % 2, :], ADD)
+            nc.scalar.activation(page[t][:].indirect(half_of(n3_t, half)), new[:], COPY)
+
+        def put(t, half):
+            nc.vector.tensor_tensor(page[t][:].indirect(half_of(n3_t, half)), old[t][:, cols_of(half)],
+                                    steps[half, t // 2][:, t % 2, :], ADD)
+
+        def finish(t):
+            nc.sync.dma_start(out_rows[:, t, :], page[t][:])
+            nc.vector.tensor_copy(planes[:, t, :], page[t][:])
+
+        hidden(0)
+        hidden(1)
+        for item in OPT["c"].split():
+            item, tag = (item + ":").split(":")[:2]
+            i, j = int(item[1]), int(item[2:] or 0)
+            if item[0] in "SV":
+                fetch(i, item[0], tag or None)
+            elif item[0] == "g":
+                gate_step(i, j)
+            elif item[0] == "n":
+                new_values(i, j)
+            elif item[0] == "p":
+                put(i, j)
+            elif item[0] == "m":
+                nc.sync.dma_start(planes[:, i, :], page[i][:])
+                nc.sync.dma_start(out_rows[:, i, :], page[i][:])
+            elif item[0] == "s":
+                nc.sync.dma_start(out_rows[:, i, :], page[i][:])
+                nc.scalar.copy(planes[:, i, :], page[i][:])
+            else:
+                finish(i)
+
+        out_w = sb("out_w", [P, U], U32)
+        out_s = sb("out_s", [P, U], U8)
+        words_hbm = out_1[0].rearrange("p c r -> p (c r)").bitcast(I32)
+        for c0 in range(0, U, CHUNK):
+            cols = slice(c0, c0 + CHUNK)
+            grouped = sb("grouped%d" % c0, [P, CHUNK, PACK], BF16)
+            dst = grouped[:].rearrange("p (c i) t -> p c t i", i=RUN)
+            src = planes[:, :, cols].rearrange("p t (c i) -> p c t i", i=RUN)
+            if c0 == U - CHUNK:
+                nc.scalar.copy(dst, src)
+            else:
+                nc.vector.tensor_copy(dst, src)
+            nc.vector.quantize_mx(out=out_w[:, cols].bitcast(FP8X4), scales=out_s[:, cols], in_=grouped[:].rearrange("p c t -> p (c t)"))
+            nc.sync.dma_start(words_hbm[:, cols], out_w[:, cols].bitcast(I32))
+        for q in range(4):
+            nc.scalar.dma_start(out_2[0].bitcast(I32)[4 * q : 4 * q + 4, :], out_s[:].bitcast(I32)[QUAD * q : QUAD * q + 4, :])

@@ -19,7 +19,7 @@ SUB = mybir.AluOpType.subtract
 SIGMOID = mybir.ActivationFunctionType.Sigmoid
 COPY = mybir.ActivationFunctionType.Copy
 
-OPT = dict(order='w1w xw w2w w3w w1s w2s mv n1 n2 w3s n3 m0 m1 m2 m3',early=[],late=[],evacS=[0],warm=0,yhold=None,w3early=1,c='S0:a0 S1:b0 V2:a1 g00 n00 n10 g10 n01 n11 m0 m1 V3:step00 g01 n30 g11 n31 p20 p21 f2 f3',hzhold='w1_raw_s')
+OPT = dict(order='w1w xw w2w w3w w1s w2s mv n1 n2 w3s n3 m0 m1 m2 m3',early=[],late=[],evacS=[0],warm=1,yhold=None,w3early=1,c='S0:a0 S1:b0 V2:a1 g00 n00 n10 g10 n01 n11 m0 m1 V3:step00 g01 n30 g11 n31 p20 p21 f2 f3',hzhold='w1_raw_s')
 P = 128
 PACK = 4
 HALF = S // 2

@@ -19,13 +19,13 @@ SUB = mybir.AluOpType.subtract
 SIGMOID = mybir.ActivationFunctionType.Sigmoid
 COPY = mybir.ActivationFunctionType.Copy
 
-OPT = dict(order='w1w xw w2w w3w w1s w2s mv n1 n2 w3s n3 m0 m1 m2 m3',early=[],late=[],evacS=[0],warm=1,yhold=None,w3early=1,c='S0:a0 S1:b0 V2:a1 g00 n00 n10 g10 n01 n11 m0 m1 V3:step00 g01 n30 g11 n31 p20 p21 f2 f3',hzhold='w1_raw_s')
+OPT = dict(order='w1w xw w2w w3w w1s w2s mv n1 n2 col w3s n3 m0 m1 m2 m3',early=[],late=[],evacS=[0],warm=1,yhold=None,w3early=1,c='S0:a0 S1:b0 V2:a1 g00 n00 n10 g10 n01 n11 m0 m1 V3:step00 g01 n30 g11 n31 p20 p21 f2 h3',hzhold='w1_raw_s',dh={(0,0):'b1'},run=2)
 P = 128
 PACK = 4
 HALF = S // 2
 QUAD = 32
 LIST_COLS = S // 16
-RUN = 4
+RUN = OPT.get("run", 2)
 CHUNK = 256
 
 
@@ -83,24 +83,18 @@ def tile_picked_twhcxbpaget_none_po_kernel(
             )
             return w
 
-        def deal_scales(name, raw_s):
+        def deal_scales(name, raw_s, engine=nc.vector):
             s = sb(name + "_s", [P, H], U8)
-            nc.vector.tensor_copy(
+            engine.tensor_copy(
                 s[:].rearrange("p (t m) -> p t m", t=PACK),
                 raw_s[:].rearrange("p (m t) -> p t m", t=PACK),
             )
             return s
 
-        def load_column(name, src):
-            tile = sb(name, [P, PACK], F32)
-            nc.gpsimd.dma_start(tile[:], src.rearrange("(p t) o -> p (t o)", t=PACK))
+        def load_column(name, src, queue=nc.gpsimd, tag=None):
+            tile = sb(name, [P, PACK], F32, tag)
+            queue.dma_start(tile[:], src.rearrange("(p t) o -> p (t o)", t=PACK))
             return tile
-
-        sl_t = load_column("sl_t", sl)
-        th_t = load_column("th_t", th)
-        sl2_t = load_column("sl2_t", sl2)
-        th2_t = load_column("th2_t", th2)
-        gn_t = load_column("gn_t", gn)
 
         def make_bias(name, slope, threshold):
             prod = sb(name + "_prod", [P, PACK], F32)
@@ -109,6 +103,10 @@ def tile_picked_twhcxbpaget_none_po_kernel(
             nc.gpsimd.tensor_scalar(bias[:], prod[:], -1.0, 0.0, MULT, ADD)
             return bias
 
+        sl_t = load_column("sl_t", sl)
+        th_t = load_column("th_t", th)
+        sl2_t = load_column("sl2_t", sl2)
+        th2_t = load_column("th2_t", th2)
         bias1 = make_bias("bias1", sl_t, th_t)
         bias2 = make_bias("bias2", sl2_t, th2_t)
         mem_rows = mem.rearrange("(p t) c -> p t c", t=PACK)
@@ -127,6 +125,8 @@ def tile_picked_twhcxbpaget_none_po_kernel(
                 nc.sync.dma_start(xw_win[:].bitcast(I32), x_words[0].rearrange("p c r -> p (c r)").bitcast(I32))
             elif item[0] == "m" and item != "mv":
                 nc.sync.dma_start(page[int(item[1])][:], mem_rows[:, int(item[1]), :])
+            elif item == "col":
+                gn_t = load_column("gn_t", gn, nc.sync)
             elif item[0] == "n":
                 L[item] = load_list(item + "_t", {"n1": n1, "n2": n2, "n3": n3}[item])
             elif item == "mv":
@@ -234,7 +234,7 @@ def tile_picked_twhcxbpaget_none_po_kernel(
             cols = cols_of(half)
             bank = h_banks[half, pair]
             gate = sb("gate%d%d" % (half, pair), [P, 2, HALF], F32)
-            diff = sb("diff%d%d" % (half, pair), [P, 2, HALF], F32, "b1" if (half, pair) == (0, 0) else None)
+            diff = sb("diff%d%d" % (half, pair), [P, 2, HALF], F32, OPT.get("dh", {}).get((half, pair)))
             step = sb("step%d%d" % (half, pair), [P, 2, HALF], F32)
             nc.scalar.activation(gate[:], bank[:], SIGMOID)
             for u in range(2):
@@ -242,14 +242,16 @@ def tile_picked_twhcxbpaget_none_po_kernel(
             nc.vector.tensor_tensor(step[:], gate[:], diff[:], MULT)
             steps[half, pair] = step
 
-        def new_values(t, half):
-            new = sb("new%d%d" % (half, t), [P, HALF], F32)
-            nc.vector.tensor_tensor(new[:], old[t][:, cols_of(half)], steps[half, t // 2][:, t % 2, :], ADD)
-            nc.scalar.activation(page[t][:].indirect(half_of(n3_t, half)), new[:], COPY)
+        def new_values(t, half, lo=0, hi=HALF):
+            c0 = half * HALF
+            new = sb("new%d%d" % (half, t), [P, hi - lo], F32)
+            nc.vector.tensor_tensor(new[:], old[t][:, c0 + lo : c0 + hi], steps[half, t // 2][:, t % 2, lo:hi], ADD)
+            nc.scalar.activation(page[t][:].indirect(n3_t[:, (c0 + lo) // 16 : (c0 + hi) // 16]), new[:], COPY)
 
-        def put(t, half):
-            nc.vector.tensor_tensor(page[t][:].indirect(half_of(n3_t, half)), old[t][:, cols_of(half)],
-                                    steps[half, t // 2][:, t % 2, :], ADD)
+        def put(t, half, lo=0, hi=HALF):
+            c0 = half * HALF
+            nc.vector.tensor_tensor(page[t][:].indirect(n3_t[:, (c0 + lo) // 16 : (c0 + hi) // 16]), old[t][:, c0 + lo : c0 + hi],
+                                    steps[half, t // 2][:, t % 2, lo:hi], ADD)
 
         def finish(t):
             nc.sync.dma_start(out_rows[:, t, :], page[t][:])
@@ -268,6 +270,14 @@ def tile_picked_twhcxbpaget_none_po_kernel(
                 new_values(i, j)
             elif item[0] == "p":
                 put(i, j)
+            elif item[0] == "N":
+                new_values(i, j, 0, HALF // 2)
+            elif item[0] == "P":
+                put(i, j, HALF // 2, HALF)
+            elif item[0] == "h":
+                nc.sync.dma_start(out_rows[:, i, :], page[i][:])
+                nc.vector.tensor_copy(planes[:, i, : U // 2], page[i][:, : U // 2])
+                nc.scalar.copy(planes[:, i, U // 2 :], page[i][:, U // 2 :])
             elif item[0] == "m":
                 nc.sync.dma_start(planes[:, i, :], page[i][:])
                 nc.sync.dma_start(out_rows[:, i, :], page[i][:])
@@ -292,4 +302,4 @@ def tile_picked_twhcxbpaget_none_po_kernel(
             nc.vector.quantize_mx(out=out_w[:, cols].bitcast(FP8X4), scales=out_s[:, cols], in_=grouped[:].rearrange("p c t -> p (c t)"))
             nc.sync.dma_start(words_hbm[:, cols], out_w[:, cols].bitcast(I32))
         for q in range(4):
-            nc.scalar.dma_start(out_2[0].bitcast(I32)[4 * q : 4 * q + 4, :], out_s[:].bitcast(I32)[QUAD * q : QUAD * q + 4, :])
+            (nc.scalar, nc.sync)[q % 2].dma_start(out_2[0].bitcast(I32)[4 * q : 4 * q + 4, :], out_s[:].bitcast(I32)[QUAD * q : QUAD * q + 4, :])

from contextlib import ExitStack

import concourse.mybir as mybir

K, T, S, N, H, U = 512, 2048, 512, 512, 512, 1024
FLOPS = 3 * 2 * 512 * 512 * 512

F32 = mybir.dt.float32
BF16 = mybir.dt.bfloat16
I32 = mybir.dt.int32
U32 = mybir.dt.uint32
U16 = mybir.dt.uint16
U8 = mybir.dt.uint8
FP8X4 = mybir.dt.float8_e4m3fn_x4
FP4X4 = mybir.dt.float4_e2m1fn_x4
MULT = mybir.AluOpType.mult
ADD = mybir.AluOpType.add
SUB = mybir.AluOpType.subtract
SIGMOID = mybir.ActivationFunctionType.Sigmoid
COPY = mybir.ActivationFunctionType.Copy

OPT = dict(order='w1w xw w2w w3w w1s w2s mv n1 n2 col w3s n3 m0 m1 m2 m3',early=[],late=[],evacS=[0],warm=1,yhold=None,w3early=1,c='S0:a0 S1:b0 V2:a1 g00 n00 n10 g10 n01 n11 m0 m1 V3:step00 g01 n30 g11 n31 p20 p21 f2 h3',hzhold='w1_raw_s',dh={(0,0):'b1'},run=2)
P = 128
PACK = 4
HALF = S // 2
QUAD = 32
LIST_COLS = S // 16
RUN = OPT.get("run", 2)
CHUNK = 256


def tile_picked_twhcxbpaget_none_po_kernel(
    tc, x_words, x_scales, w1_words, w1_scales, w2_words, w2_scales, sl, th, sl2, th2, gn,
    w3_words, w3_scales, mem, offs, hz, n1, n2, n3, out_0, out_1, out_2,
):
    nc = tc.nc
    with ExitStack() as ctx:
        keep = ctx.enter_context(tc.tile_pool(name="keep", bufs=1))
        psum = ctx.enter_context(tc.psum_pool(name="psum", bufs=8))

        def sb(name, shape, dtype, tag=None):
            return keep.tile(shape, dtype, name=name, tag=tag or name, align_bytes=64)

        def load_list(name, src):
            tile = sb(name, [P, LIST_COLS], U16)
            nc.sync.dma_start(tile[:], src)
            return tile

        def half_of(lst, half):
            return lst[:, half * (LIST_COLS // 2) : (half + 1) * (LIST_COLS // 2)]

        def cols_of(half):
            return slice(half * HALF, (half + 1) * HALF)

        xs_win = sb("xs_win", [P, T], U8)
        nc.gpsimd.memset(xs_win[:].bitcast(I32), 0)
        hz_t = load_list("hz_t", hz)
        offs_t = load_list("offs_t", offs)
        xs_rows = x_scales[0].bitcast(I32)
        xs_i32 = xs_win[:].bitcast(I32)
        for e in range(2):
            nc.sync.dma_start(xs_i32[e:P:16, :], xs_rows[e:16:2, :])
        for e in range(2):
            nc.sync.dma_start(xs_i32[2 + e : P : QUAD, :], xs_rows[2 + e : 16 : 4, :])

        def load_words(name, words, queue, tag):
            raw_w = sb(name + "_raw_w", [P, 2 * H], U8, tag)
            queue.dma_start(raw_w[:].bitcast(I32), words[0].bitcast(I32))
            return raw_w

        def load_scales(name, scales, queue, tag):
            raw_s = sb(name + "_raw_s", [P, H], U8, tag)
            nc.vector.memset(raw_s[:].bitcast(I32), 0)
            for r in range(4):
                queue.dma_start(raw_s[:].bitcast(I32)[r:P:QUAD, :], scales[0].bitcast(I32)[r:16:4, :])
            return raw_s

        def deal_words(name, raw_w):
            w = sb(name + "_w", [P, 2 * H], U8)
            nc.scalar.copy(
                w[:].bitcast(U16).rearrange("p (t m) -> p t m", t=PACK),
                raw_w[:].bitcast(U16).rearrange("p (m t) -> p t m", t=PACK),
            )
            return w

        def deal_scales(name, raw_s, engine=nc.vector):
            s = sb(name + "_s", [P, H], U8)
            engine.tensor_copy(
                s[:].rearrange("p (t m) -> p t m", t=PACK),
                raw_s[:].rearrange("p (m t) -> p t m", t=PACK),
            )
            return s

        def load_column(name, src, queue=nc.gpsimd, tag=None):
            tile = sb(name, [P, PACK], F32, tag)
            queue.dma_start(tile[:], src.rearrange("(p t) o -> p (t o)", t=PACK))
            return tile

        def make_bias(name, slope, threshold):
            prod = sb(name + "_prod", [P, PACK], F32)
            bias = sb(name, [P, PACK], F32)
            nc.gpsimd.tensor_tensor(prod[:], slope[:], threshold[:], MULT)
            nc.gpsimd.tensor_scalar(bias[:], prod[:], -1.0, 0.0, MULT, ADD)
            return bias

        sl_t = load_column("sl_t", sl)
        th_t = load_column("th_t", th)
        sl2_t = load_column("sl2_t", sl2)
        th2_t = load_column("th2_t", th2)
        bias1 = make_bias("bias1", sl_t, th_t)
        bias2 = make_bias("bias2", sl2_t, th2_t)
        mem_rows = mem.rearrange("(p t) c -> p t c", t=PACK)
        out_rows = out_0.rearrange("(p t) c -> p t c", t=PACK)
        page = [sb("page%d" % t, [P, U], F32) for t in range(PACK)]
        xw_win = sb("xw_win", [P, T], U32)
        hz_s_raw = sb("hz_s_raw", [P, S], U8)
        hz_s = sb("hz_s", [P, S], U8)
        L = {}
        if OPT.get("warm"):
            warm = sb("warm", [P, 8], F32)
            nc.vector.memset(warm[:, 0:1], 0.0)
            nc.scalar.activation(warm[:, 1:2], warm[:, 0:1], SIGMOID)
        for item in OPT["order"].split():
            if item == "xw":
                nc.sync.dma_start(xw_win[:].bitcast(I32), x_words[0].rearrange("p c r -> p (c r)").bitcast(I32))
            elif item[0] == "m" and item != "mv":
                nc.sync.dma_start(page[int(item[1])][:], mem_rows[:, int(item[1]), :])
            elif item == "col":
                gn_t = load_column("gn_t", gn, nc.sync)
            elif item[0] == "n":
                L[item] = load_list(item + "_t", {"n1": n1, "n2": n2, "n3": n3}[item])
            elif item == "mv":
                nc.vector.tensor_copy(hz_s_raw[:], xs_win[:].indirect(hz_t[:]))
                nc.vector.tensor_copy(hz_s[:].bitcast(I32), hz_s_raw[:].bitcast(I32))
                for e in range(2):
                    nc.sync.dma_start(hz_s[:].bitcast(I32)[2 + e : P : QUAD, :], hz_s_raw[:].bitcast(I32)[16 + e : P : QUAD, :])
            elif item[2] == "w":
                L[item] = load_words(item[:2], {"w1": w1_words, "w2": w2_words, "w3": w3_words}[item[:2]], nc.sync, None)
            else:
                L[item] = load_scales(item[:2], {"w1": w1_scales, "w2": w2_scales, "w3": w3_scales}[item[:2]], nc.sync, None)
        n1_t, n2_t, n3_t = L["n1"], L["n2"], L["n3"]
        raw1_w, raw2_w, raw3_w, raw1_s, raw2_s, raw3_s = L["w1w"], L["w2w"], L["w3w"], L["w1s"], L["w2s"], L["w3s"]

        tok_s = sb("tok_s", [P, S], U8)
        nc.vector.tensor_copy(tok_s[:], xs_win[:].indirect(offs_t[:]))
        tok_w = sb("tok_w", [P, S], U32)
        nc.vector.tensor_copy(tok_w[:], xw_win[:].indirect(offs_t[:]))
        old = {}
        w1 = (deal_words("w1", raw1_w), deal_scales("w1", raw1_s))
        w2 = (deal_words("w2", raw2_w), deal_scales("w2", raw2_s))
        hz_w = sb("hz_w", [P, S], U32, OPT.get("hzhold", "w2_raw_s"))
        nc.vector.tensor_copy(hz_w[:], xw_win[:].indirect(hz_t[:]))
        if OPT.get("w3early"):
            w3_w = deal_words("w3", raw3_w)
        olds = {}

        def fetch(t, eng, tag=None):
            old[t] = sb("old%d" % t, [P, S], F32, tag)
            if eng == "S":
                nc.scalar.activation(old[t][:], page[t][:].indirect(n3_t[:]), COPY)
            else:
                nc.vector.tensor_copy(old[t][:], page[t][:].indirect(n3_t[:]))

        for t in OPT["early"]:
            fetch(t, "S")

        def product(out, weight, t, codes, scales):
            w, s = weight
            nc.tensor.matmul_mx(
                out=out,
                lhsT=w[:, 2 * P * t : 2 * P * (t + 1)].bitcast(FP4X4),
                lhsT_scale=s[:, P * t : P * (t + 1)],
                rhs=codes.bitcast(FP8X4),
                rhs_scale=scales,
                start=True,
                stop=True,
            )

        y = [sb("y%d" % t, [P, S], F32, "w2_raw_s" if t == OPT.get("yhold") else None) for t in range(PACK)]
        d = [sb("d%d" % t, [P, S], F32) for t in range(PACK)]
        for t in range(PACK):
            bank = psum.tile([P, S], F32, tag="bank", name="y_bank")
            product(bank[:], w1, t, tok_w[:], tok_s[:])
            if t in OPT["evacS"]:
                nc.scalar.copy(y[t][:], bank[:])
            else:
                nc.vector.tensor_copy(y[t][:], bank[:])
        for t in range(PACK):
            bank = psum.tile([P, S], F32, tag="bank", name="d_bank")
            product(bank[:], w2, t, hz_w[:], hz_s[:])
            nc.vector.tensor_copy(d[t][:], bank[:])
        if not OPT.get("w3early"):
            w3_w = deal_words("w3", raw3_w)
        w3 = (w3_w, deal_scales("w3", raw3_s))
        sg = sb("sg", [P, PACK, HALF], F32)
        sg2 = sb("sg2", [P, PACK, HALF], F32)

        h_banks = {}

        def hidden(half):
            cols = cols_of(half)
            a = sb("a%d" % half, [P, PACK, HALF], F32)
            b = sb("b%d" % half, [P, PACK, HALF], F32)
            for t in range(PACK):
                nc.scalar.activation(sg[:, t, :], y[t][:].indirect(half_of(n1_t, half)), SIGMOID,
                                     bias=bias1[:, t : t + 1], scale=sl_t[:, t : t + 1])
            for t in range(PACK):
                nc.scalar.activation(sg2[:, t, :], d[t][:].indirect(half_of(n2_t, half)), SIGMOID,
                                     bias=bias2[:, t : t + 1], scale=sl2_t[:, t : t + 1])
            for t in range(PACK):
                nc.vector.scalar_tensor_tensor(a[:, t, :], sg[:, t, :], gn_t[:, t : t + 1], d[t][:, cols], MULT, MULT)
            for t in range(PACK):
                nc.vector.scalar_tensor_tensor(b[:, t, :], sg2[:, t, :], gn_t[:, t : t + 1], y[t][:, cols], MULT, MULT)
            z = sb("z%d" % half, [P, HALF, PACK], BF16)
            nc.vector.tensor_tensor(
                z[:].rearrange("p (c i) t -> p c t i", i=RUN),
                a[:].rearrange("p t (c i) -> p c t i", i=RUN),
                b[:].rearrange("p t (c i) -> p c t i", i=RUN),
                ADD,
            )
            z_w = sb("z_w%d" % half, [P, HALF], U32)
            z_s = sb("z_s%d" % half, [P, HALF], U8)
            nc.vector.quantize_mx(out=z_w[:].bitcast(FP8X4), scales=z_s[:], in_=z[:].rearrange("p c t -> p (c t)"))
            for pair in range(2):
                bank = psum.tile([P, 2, HALF], F32, tag="bank", name="h_bank")
                for u in range(2):
                    product(bank[:, u, :], w3, 2 * pair + u, z_w[:], z_s[:])
                h_banks[half, pair] = bank

        planes = sb("planes", [P, PACK, U], F32)
        steps = {}

        def gate_step(half, pair):
            cols = cols_of(half)
            bank = h_banks[half, pair]
            gate = sb("gate%d%d" % (half, pair), [P, 2, HALF], F32)
            diff = sb("diff%d%d" % (half, pair), [P, 2, HALF], F32, OPT.get("dh", {}).get((half, pair)))
            step = sb("step%d%d" % (half, pair), [P, 2, HALF], F32)
            nc.scalar.activation(gate[:], bank[:], SIGMOID)
            for u in range(2):
                nc.vector.tensor_tensor(diff[:, u, :], bank[:, u, :], old[2 * pair + u][:, cols], SUB)
            nc.vector.tensor_tensor(step[:], gate[:], diff[:], MULT)
            steps[half, pair] = step

        def new_values(t, half, lo=0, hi=HALF):
            c0 = half * HALF
            new = sb("new%d%d" % (half, t), [P, hi - lo], F32)
            nc.vector.tensor_tensor(new[:], old[t][:, c0 + lo : c0 + hi], steps[half, t // 2][:, t % 2, lo:hi], ADD)
            nc.scalar.activation(page[t][:].indirect(n3_t[:, (c0 + lo) // 16 : (c0 + hi) // 16]), new[:], COPY)

        def put(t, half, lo=0, hi=HALF):
            c0 = half * HALF
            nc.vector.tensor_tensor(page[t][:].indirect(n3_t[:, (c0 + lo) // 16 : (c0 + hi) // 16]), old[t][:, c0 + lo : c0 + hi],
                                    steps[half, t // 2][:, t % 2, lo:hi], ADD)

        def finish(t):
            nc.sync.dma_start(out_rows[:, t, :], page[t][:])
            nc.vector.tensor_copy(planes[:, t, :], page[t][:])

        hidden(0)
        hidden(1)
        for item in OPT["c"].split():
            item, tag = (item + ":").split(":")[:2]
            i, j = int(item[1]), int(item[2:] or 0)
            if item[0] in "SV":
                fetch(i, item[0], tag or None)
            elif item[0] == "g":
                gate_step(i, j)
            elif item[0] == "n":
                new_values(i, j)
            elif item[0] == "p":
                put(i, j)
            elif item[0] == "N":
                new_values(i, j, 0, HALF // 2)
            elif item[0] == "P":
                put(i, j, HALF // 2, HALF)
            elif item[0] == "h":
                nc.sync.dma_start(out_rows[:, i, :], page[i][:])
                nc.vector.tensor_copy(planes[:, i, : U // 2], page[i][:, : U // 2])
                nc.scalar.copy(planes[:, i, U // 2 :], page[i][:, U // 2 :])
            elif item[0] == "m":
                nc.sync.dma_start(planes[:, i, :], page[i][:])
                nc.sync.dma_start(out_rows[:, i, :], page[i][:])
            elif item[0] == "s":
                nc.sync.dma_start(out_rows[:, i, :], page[i][:])
                nc.scalar.copy(planes[:, i, :], page[i][:])
            else:
                finish(i)

        out_w = sb("out_w", [P, U], U32)
        out_s = sb("out_s", [P, U], U8)
        words_hbm = out_1[0].rearrange("p c r -> p (c r)").bitcast(I32)
        for c0 in range(0, U, CHUNK):
            cols = slice(c0, c0 + CHUNK)
            grouped = sb("grouped%d" % c0, [P, CHUNK, PACK], BF16)
            dst = grouped[:].rearrange("p (c i) t -> p c t i", i=RUN)
            src = planes[:, :, cols].rearrange("p t (c i) -> p c t i", i=RUN)
            if c0 == U - CHUNK:
                nc.scalar.copy(dst, src)
            else:
                nc.vector.tensor_copy(dst, src)
            nc.vector.quantize_mx(out=out_w[:, cols].bitcast(FP8X4), scales=out_s[:, cols], in_=grouped[:].rearrange("p c t -> p (c t)"))
            nc.sync.dma_start(words_hbm[:, cols], out_w[:, cols].bitcast(I32))
        for q in range(4):
            (nc.scalar, nc.sync)[q % 2].dma_start(out_2[0].bitcast(I32)[4 * q : 4 * q + 4, :], out_s[:].bitcast(I32)[QUAD * q : QUAD * q + 4, :])
